import numpy as np
import ml_dtypes


def mxq(x, axis, fmt="e4m3"):
    dtype, down = {"e4m3": (ml_dtypes.float8_e4m3fn, 7), "e5m2": (ml_dtypes.float8_e5m2, 14)}[fmt]
    v = np.moveaxis(np.asarray(x, np.float32).astype(ml_dtypes.bfloat16).astype(np.float64), axis, -1)
    blocks = v.reshape(v.shape[:-1] + (-1, 32))
    amax = np.abs(blocks).max(-1, keepdims=True)
    byte = np.maximum(np.where(amax > 0, np.frexp(amax)[1] - 1 + 127, 0) - down, 1)
    scale = np.exp2(byte - 127.0)
    codes = (blocks / scale).astype(np.float32).astype(dtype).astype(np.float64)
    return np.moveaxis((codes * scale).reshape(v.shape), -1, axis)


WIDE = False


def mx_kscale(k):
    if not WIDE:
        return np.ones(k)
    levels = np.array([10, -10, 5, -5, 0])
    if k % 512:
        return np.exp2(np.random.permutation(np.resize(levels, k // 32))).repeat(32)
    a = np.empty((k // 512, 16))
    for p in range(k // 512):
        a[p, :8] = np.random.permutation(np.resize(levels, 8))
        for g in range(8):
            far = levels[np.abs(levels - a[p, g]) >= 10]
            a[p, g + 8] = far[np.random.randint(len(far))]
    return np.exp2(a.ravel()).repeat(32)


def f64(x):
    return np.asarray(x).astype(np.float64)


def striped(idx):
    return np.tile(idx.reshape(-1, 16).T, (8, 1)).astype(np.uint16)


def unstriped(offs):
    return offs[:16].T.reshape(-1).astype(np.int64)


def pack_weight(w):
    k, n = w.shape
    w = f64(np.asarray(w, np.float32).astype(ml_dtypes.bfloat16)).reshape(k // 32, 32, n)
    amax = np.abs(w).max(1)
    byte = np.clip(np.where(amax > 0, np.frexp(amax)[1] - 1 + 127 - 7, 1), 1, 254)
    scaled = (w * np.exp2(127.0 - byte)[:, None, :]).reshape(k, n).astype(np.float32)
    words = np.ascontiguousarray(scaled.reshape(k // 512, 128, 4, n).transpose(0, 1, 3, 2)).astype(ml_dtypes.float8_e4m3fn).view(np.uint8)
    return words, np.ascontiguousarray(byte.astype(np.uint8).reshape(k // 512, 16, n))


def unpack_weight(words, scales):
    g, p, n, _ = words.shape
    vals = np.ascontiguousarray(words).view(ml_dtypes.float8_e4m3fn).astype(np.float64) * np.repeat(np.exp2(scales.astype(np.float64) - 127.0), 8, axis=1)[..., None]
    return vals.transpose(0, 1, 3, 2).reshape(g * 512, n)


K, T, E, C, N = 1024, 512, 4, 128, 128


def by_expert(wq, xq):
    return np.concatenate([wq[e].T @ xq[:, e * C:(e + 1) * C] for e in range(E)], axis=1)


def setup_inputs():
    n = np.random.standard_normal
    s = mx_kscale(K)[:, None]
    packed = [pack_weight(m) for m in n((E, K, N)) / np.sqrt(K) / s[None]]
    return {
        "xT": (n((K, T)) * s).astype(np.float32),
        "w_words": np.stack([m[0] for m in packed]),
        "w_scales": np.stack([m[1] for m in packed]),
        "offs": striped(np.random.permutation(T)[:E * C]),
    }


def reference(xT, w_words, w_scales, offs):
    idx = unstriped(offs)
    xq = mxq(f64(xT)[:, idx], 0, "e4m3")
    w = np.stack([unpack_weight(w_words[e], w_scales[e]) for e in range(E)])
    y = by_expert(w, xq)
    out = np.zeros((N, T))
    out[:, idx] = y
    return out

@@ -1,0 +1,135 @@
+import concourse.mybir as mybir
+
+FLOPS = 2 * 1024 * 128 * 512
+
+F32 = mybir.dt.float32
+BF16 = mybir.dt.bfloat16
+I32 = mybir.dt.int32
+U32 = mybir.dt.uint32
+U16 = mybir.dt.uint16
+U8 = mybir.dt.uint8
+FP8X4 = mybir.dt.float8_e4m3fn_x4
+COPY = mybir.ActivationFunctionType.Copy
+
+P = 128
+T = 512
+E = 4
+C = 128
+N = 128
+PASSES = 2
+HALF = 256
+PIECES = ((0, 0), (1, 0), (1, 1), (0, 1))
+SLOTS = len(PIECES)
+EARLY = PIECES[1][0]
+LATE = PIECES[3][0]
+CASTS = [[[0,176,80],[256,176,80]],[[0,192,320]],[[0,0,512]],[[0,0,512]]]
+
+
+def tile_routed_moe_kernel(tc, xT, w_words, w_scales, offs, out):
+    nc = tc.nc
+    with (
+        tc.tile_pool(name="keep", bufs=1) as keep,
+        tc.psum_pool(name="psum", bufs=1) as psum,
+    ):
+        lists = keep.tile([P, T // 16], U16, name="lists")
+        x_view = xT.rearrange("(g p u e) n -> g u p e n", g=PASSES, p=P, u=2, e=2)
+        raw = [keep.tile([P, 2, T], F32, name="raw%d" % i) for i in range(SLOTS)]
+        first = x_view[PIECES[0][0], PIECES[0][1]]
+        nc.sync.dma_start(raw[0][:, :, 0:HALF], first[:, :, 0:HALF])
+        nc.sync.dma_start(raw[0][:, :, HALF:T], first[:, :, HALF:T])
+        nc.sync.dma_start(lists[:], offs)
+        for i in range(1, SLOTS):
+            nc.sync.dma_start(raw[i][:], x_view[PIECES[i][0], PIECES[i][1]])
+
+        warm_in = keep.tile([P, 1], F32, name="warm_in")
+        warm_out = keep.tile([P, 1], F32, name="warm_out")
+        nc.vector.memset(warm_in[:], 0.0)
+        nc.scalar.copy(out=warm_out[:], in_=warm_in[:])
+
+        w_scale_sb = keep.tile([P, E * PASSES, N], U8, name="w_scale_sb", align_bytes=64)
+        nc.vector.memset(w_scale_sb[:].rearrange("p i n -> p (i n)").bitcast(I32), 0)
+        s_view = w_scales.rearrange("e a (q r) n -> r q (e a) n", r=4)
+        for r in range(4):
+            nc.sync.dma_start(w_scale_sb[r:P:32, :, :].bitcast(I32), s_view[r].bitcast(I32))
+        w_code_sb = keep.tile([P, E * PASSES, 4 * N], U8, name="w_code_sb", align_bytes=64)
+        nc.sync.dma_start(w_code_sb[:], w_words.rearrange("e a p n r -> p (e a) (n r)"))
+
+        pairs = keep.tile([P, SLOTS + 1, T, 2], BF16, name="pairs")
+        nc.vector.memset(pairs[:, SLOTS, :, :], 0.0)
+        pair_words = pairs[:].rearrange("p i n e -> p (i n e)").bitcast(U32)
+        planes = keep.tile([P, 2, T], BF16, name="planes")
+        plain = [keep.tile([P, 2, T, 2], BF16, name="plain%d" % g) for g in range(PASSES)]
+        grouped = [keep.tile([P, T, 4], BF16, name="grouped%d" % g, align_bytes=64) for g in range(PASSES)]
+        x_code = [keep.tile([P, T], U32, name="x_code%d" % g, align_bytes=64) for g in range(PASSES)]
+        x_scale = [keep.tile([P, T], U8, name="x_scale%d" % g, align_bytes=64) for g in range(PASSES)]
+        acc = [psum.tile([P, C], F32, name="acc%d" % e) for e in range(E)]
+        y = [keep.tile([P, HALF], F32, name="y%d" % h) for h in range(2)]
+        window_out = keep.tile([P, T], F32, name="window_out")
+
+        def cast(i):
+            slot = SLOTS - 1 - i
+            for start, for_vector, for_scalar in CASTS[i]:
+                for engine, a, b in (
+                    (nc.vector.tensor_copy, start, start + for_vector),
+                    (nc.scalar.copy, start + for_vector, start + for_vector + for_scalar),
+                ):
+                    if b > a:
+                        engine(
+                            out=pairs[:, slot, a:b, :].rearrange("p (c i) e -> p c e i", i=4),
+                            in_=raw[i][:, :, a:b].rearrange("p e (c i) -> p c e i", i=4),
+                        )
+
+        def gather(i, start, count, width):
+            slot = SLOTS - 1 - i
+            words = plain[PIECES[i][0]][:, PIECES[i][1], :, :].rearrange("p s e -> p (s e)").bitcast(U32)
+            nc.vector.tensor_copy(
+                words[:, start:start + count],
+                pair_words[:, slot * T:slot * T + width].indirect(lists[:, start // 16:(start + count) // 16]),
+            )
+
+        def quantize(g, start, count):
+            cols = slice(start, start + count)
+            nc.vector.tensor_copy(
+                out=grouped[g][:, cols, :].rearrange("p s t -> p (s t)").bitcast(I32).rearrange("p (s u) -> p s u", u=2),
+                in_=plain[g][:].rearrange("p u s e -> p (u s e)").bitcast(I32).rearrange("p (u s) -> p s u", u=2)[:, cols, :],
+            )
+            nc.vector.quantize_mx(
+                out=x_code[g][:, cols].bitcast(FP8X4),
+                scales=x_scale[g][:, cols],
+                in_=grouped[g][:, cols, :].rearrange("p s t -> p (s t)"),
+            )
+
+        def multiply(e, a, start, stop):
+            nc.tensor.matmul_mx(
+                out=acc[e][:],
+                lhsT=w_code_sb[:, e * PASSES + a, :].bitcast(FP8X4),
+                lhsT_scale=w_scale_sb[:, e * PASSES + a, :],
+                rhs=x_code[a][:, e * C:(e + 1) * C].bitcast(FP8X4),
+                rhs_scale=x_scale[a][:, e * C:(e + 1) * C],
+                start=start,
+                stop=stop,
+            )
+
+        for i in range(3):
+            cast(i)
+            gather(i, 0, T, 2 * T)
+        nc.scalar.copy(out=planes[:], in_=raw[3][:])
+        quantize(EARLY, 0, T)
+        for e in range(E):
+            multiply(e, EARLY, True, False)
+        for h in range(2):
+            for e in range(2):
+                nc.scalar.activation(
+                    plain[LATE][:, PIECES[3][1], h * HALF:(h + 1) * HALF, e],
+                    planes[:, e, :].indirect(lists[:, h * (HALF // 16):(h + 1) * (HALF // 16)]),
+                    COPY,
+                )
+            quantize(LATE, h * HALF, HALF)
+        for e in range(E):
+            multiply(e, LATE, False, True)
+            nc.scalar.copy(out=y[e // 2][:, (e % 2) * C:(e % 2 + 1) * C], in_=acc[e][:])
+        for h in range(2):
+            nc.vector.tensor_copy(
+                window_out[:].indirect(lists[:, h * (HALF // 16):(h + 1) * (HALF // 16)]), y[h][:]
+            )
+        nc.sync.dma_start(out, window_out[:])

@@ -81,7 +81,10 @@ def tile_routed_moe_kernel(tc, xT, w_words, w_scales, offs, out):
 
         def gather(i, start, count, width):
             slot = SLOTS - 1 - i
-            words = plain[PIECES[i][0]][:, PIECES[i][1], :, :].rearrange("p s e -> p (s e)").bitcast(U32)
+            if PIECES[i][0] == LATE:
+                words = grouped[LATE][:].rearrange("p s t -> p (s t)").bitcast(U32).rearrange("p (s u) -> p s u", u=2)[:, :, PIECES[i][1]]
+            else:
+                words = plain[PIECES[i][0]][:, PIECES[i][1], :, :].rearrange("p s e -> p (s e)").bitcast(U32)
             nc.vector.tensor_copy(
                 words[:, start:start + count],
                 pair_words[:, slot * T:slot * T + width].indirect(lists[:, start // 16:(start + count) // 16]),
@@ -89,10 +92,11 @@ def tile_routed_moe_kernel(tc, xT, w_words, w_scales, offs, out):
 
         def quantize(g, start, count):
             cols = slice(start, start + count)
-            nc.vector.tensor_copy(
+            if g == EARLY:
+              nc.vector.tensor_copy(
                 out=grouped[g][:, cols, :].rearrange("p s t -> p (s t)").bitcast(I32).rearrange("p (s u) -> p s u", u=2),
                 in_=plain[g][:].rearrange("p u s e -> p (u s e)").bitcast(I32).rearrange("p (u s) -> p s u", u=2)[:, cols, :],
-            )
+              )
             nc.vector.quantize_mx(
                 out=x_code[g][:, cols].bitcast(FP8X4),
                 scales=x_scale[g][:, cols],
@@ -120,7 +124,7 @@ def tile_routed_moe_kernel(tc, xT, w_words, w_scales, offs, out):
         for h in range(2):
             for e in range(2):
                 nc.scalar.activation(
-                    plain[LATE][:, PIECES[3][1], h * HALF:(h + 1) * HALF, e],
+                    grouped[LATE][:, h * HALF:(h + 1) * HALF, 2 * PIECES[3][1] + e],
                     planes[:, e, :].indirect(lists[:, h * (HALF // 16):(h + 1) * (HALF // 16)]),
                     COPY,
                 )

@@ -23,6 +23,7 @@ SLOTS = len(PIECES)
 EARLY = PIECES[1][0]
 LATE = PIECES[3][0]
 CASTS = [[[0,176,80],[256,176,80]],[[0,192,320]],[[0,0,512]],[[0,0,512]]]
+PLANES_FOR_VECTOR = 224
 
 
 def tile_routed_moe_kernel(tc, xT, w_words, w_scales, offs, out):
@@ -117,7 +118,11 @@ def tile_routed_moe_kernel(tc, xT, w_words, w_scales, offs, out):
         for i in range(3):
             cast(i)
             gather(i, 0, T, 2 * T)
-        nc.scalar.copy(out=planes[:], in_=raw[3][:])
+        nc.gpsimd.tensor_scalar(
+            out=planes[:, :, 0:PLANES_FOR_VECTOR], in0=raw[3][:, :, 0:PLANES_FOR_VECTOR],
+            scalar1=1.0, scalar2=0.0, op0=mybir.AluOpType.mult, op1=mybir.AluOpType.add,
+        )
+        nc.scalar.copy(out=planes[:, :, PLANES_FOR_VECTOR:T], in_=raw[3][:, :, PLANES_FOR_VECTOR:T])
         quantize(EARLY, 0, T)
         for e in range(E):
             multiply(e, EARLY, True, False)

@@ -39,8 +39,10 @@ def tile_routed_moe_kernel(tc, xT, w_words, w_scales, offs, out):
         nc.sync.dma_start(raw[0][:, :, 0:HALF], first[:, :, 0:HALF])
         nc.sync.dma_start(raw[0][:, :, HALF:T], first[:, :, HALF:T])
         nc.sync.dma_start(lists[:], offs)
-        for i in range(1, SLOTS):
+        for i in range(1, SLOTS - 1):
             nc.sync.dma_start(raw[i][:], x_view[PIECES[i][0], PIECES[i][1]])
+        for v in range(2):
+            nc.sync.dma_start(raw[3][:, v, :], x_view[PIECES[3][0], PIECES[3][1]][:, v, :])
 
         warm_in = keep.tile([P, 1], F32, name="warm_in")
         warm_out = keep.tile([P, 1], F32, name="warm_out")
@@ -91,13 +93,15 @@ def tile_routed_moe_kernel(tc, xT, w_words, w_scales, offs, out):
                 pair_words[:, slot * T:slot * T + width].indirect(lists[:, start // 16:(start + count) // 16]),
             )
 
-        def quantize(g, start, count):
+        def interleave(g, start, count):
             cols = slice(start, start + count)
-            if g == EARLY:
-              nc.vector.tensor_copy(
+            nc.vector.tensor_copy(
                 out=grouped[g][:, cols, :].rearrange("p s t -> p (s t)").bitcast(I32).rearrange("p (s u) -> p s u", u=2),
                 in_=plain[g][:].rearrange("p u s e -> p (u s e)").bitcast(I32).rearrange("p (u s) -> p s u", u=2)[:, cols, :],
-              )
+            )
+
+        def quantize(g, start, count):
+            cols = slice(start, start + count)
             nc.vector.quantize_mx(
                 out=x_code[g][:, cols].bitcast(FP8X4),
                 scales=x_scale[g][:, cols],
@@ -118,19 +122,24 @@ def tile_routed_moe_kernel(tc, xT, w_words, w_scales, offs, out):
         for i in range(3):
             cast(i)
             gather(i, 0, T, 2 * T)
-        nc.gpsimd.tensor_scalar(
-            out=planes[:, :, 0:PLANES_FOR_VECTOR], in0=raw[3][:, :, 0:PLANES_FOR_VECTOR],
-            scalar1=1.0, scalar2=0.0, op0=mybir.AluOpType.mult, op1=mybir.AluOpType.add,
-        )
-        nc.scalar.copy(out=planes[:, :, PLANES_FOR_VECTOR:T], in_=raw[3][:, :, PLANES_FOR_VECTOR:T])
-        quantize(EARLY, 0, T)
-        for e in range(E):
-            multiply(e, EARLY, True, False)
+        def by_gpsimd(out, in_):
+            nc.gpsimd.tensor_scalar(out=out, in0=in_, scalar1=1.0, scalar2=0.0, op0=mybir.AluOpType.mult, op1=mybir.AluOpType.add)
+
+        by_gpsimd(planes[:, 0, 0:288], raw[3][:, 0, 0:288])
+        nc.scalar.copy(out=planes[:, 0, 288:T], in_=raw[3][:, 0, 288:T])
+        by_gpsimd(planes[:, 1, :], raw[3][:, 1, :])
         for h in range(2):
-            for e in range(2):
+            interleave(EARLY, h * HALF, HALF)
+        for h in range(2):
+            quantize(EARLY, h * HALF, HALF)
+            for e in (2 * h, 2 * h + 1):
+                multiply(e, EARLY, True, False)
+        both_planes = planes[:].rearrange("p v n -> p (v n)")
+        for h in range(2):
+            for v in range(2):
                 nc.scalar.activation(
-                    grouped[LATE][:, h * HALF:(h + 1) * HALF, 2 * PIECES[3][1] + e],
-                    planes[:, e, :].indirect(lists[:, h * (HALF // 16):(h + 1) * (HALF // 16)]),
+                    grouped[LATE][:, h * HALF:(h + 1) * HALF, 2 * PIECES[3][1] + v],
+                    (both_planes if (h, v) == (1, 0) else planes[:, v, :]).indirect(lists[:, h * (HALF // 16):(h + 1) * (HALF // 16)]),
                     COPY,
                 )
             quantize(LATE, h * HALF, HALF)

@@ -22,7 +22,8 @@ PIECES = ((0, 0), (1, 0), (1, 1), (0, 1))
 SLOTS = len(PIECES)
 EARLY = PIECES[1][0]
 LATE = PIECES[3][0]
-CASTS = [[[0,176,80],[256,176,80]],[[0,192,320]],[[0,0,512]],[[0,0,512]]]
+CASTS = [[[0,176,80,0],[256,176,80,0]],[[0,0,384,128]],[[0,0,368,144]]]
+PLANE0_FOR_GPSIMD = 304
 PLANES_FOR_VECTOR = 224
 
 
@@ -69,12 +70,16 @@ def tile_routed_moe_kernel(tc, xT, w_words, w_scales, offs, out):
         y = [keep.tile([P, HALF], F32, name="y%d" % h) for h in range(2)]
         window_out = keep.tile([P, T], F32, name="window_out")
 
+        def by_gpsimd(out, in_):
+            nc.gpsimd.tensor_scalar(out=out, in0=in_, scalar1=1.0, scalar2=0.0, op0=mybir.AluOpType.mult, op1=mybir.AluOpType.add)
+
         def cast(i):
             slot = SLOTS - 1 - i
-            for start, for_vector, for_scalar in CASTS[i]:
+            for start, for_vector, for_scalar, for_gpsimd in CASTS[i]:
                 for engine, a, b in (
                     (nc.vector.tensor_copy, start, start + for_vector),
                     (nc.scalar.copy, start + for_vector, start + for_vector + for_scalar),
+                    (by_gpsimd, start + for_vector + for_scalar, start + for_vector + for_scalar + for_gpsimd),
                 ):
                     if b > a:
                         engine(
@@ -122,11 +127,8 @@ def tile_routed_moe_kernel(tc, xT, w_words, w_scales, offs, out):
         for i in range(3):
             cast(i)
             gather(i, 0, T, 2 * T)
-        def by_gpsimd(out, in_):
-            nc.gpsimd.tensor_scalar(out=out, in0=in_, scalar1=1.0, scalar2=0.0, op0=mybir.AluOpType.mult, op1=mybir.AluOpType.add)
-
-        by_gpsimd(planes[:, 0, 0:288], raw[3][:, 0, 0:288])
-        nc.scalar.copy(out=planes[:, 0, 288:T], in_=raw[3][:, 0, 288:T])
+        by_gpsimd(planes[:, 0, 0:PLANE0_FOR_GPSIMD], raw[3][:, 0, 0:PLANE0_FOR_GPSIMD])
+        nc.scalar.copy(out=planes[:, 0, PLANE0_FOR_GPSIMD:T], in_=raw[3][:, 0, PLANE0_FOR_GPSIMD:T])
         by_gpsimd(planes[:, 1, :], raw[3][:, 1, :])
         for h in range(2):
             interleave(EARLY, h * HALF, HALF)

@@ -10,6 +10,8 @@ U16 = mybir.dt.uint16
 U8 = mybir.dt.uint8
 FP8X4 = mybir.dt.float8_e4m3fn_x4
 COPY = mybir.ActivationFunctionType.Copy
+MULT = mybir.AluOpType.mult
+ADD = mybir.AluOpType.add
 
 P = 128
 T = 512
@@ -17,14 +19,18 @@ E = 4
 C = 128
 N = 128
 PASSES = 2
-HALF = 256
-PIECES = ((0, 0), (1, 0), (1, 1), (0, 1))
-SLOTS = len(PIECES)
-EARLY = PIECES[1][0]
-LATE = PIECES[3][0]
-CASTS = [[[0,176,80,0],[256,176,80,0]],[[0,0,384,128]],[[0,0,368,144]]]
+HALF = T // 2
+
+EARLY, LATE = 1, 0
+PAIR_PIECES = ((LATE, 0), (EARLY, 0), (EARLY, 1))
+PLANE_PIECE = (LATE, 1)
+
+PAIR_CASTS = (
+    (("vector", 0, 176), ("scalar", 176, 80), ("vector", 256, 176), ("scalar", 432, 80)),
+    (("scalar", 0, 384), ("gpsimd", 384, 128)),
+    (("scalar", 0, 368), ("gpsimd", 368, 144)),
+)
 PLANE0_FOR_GPSIMD = 304
-PLANES_FOR_VECTOR = 224
 
 
 def tile_routed_moe_kernel(tc, xT, w_words, w_scales, offs, out):
@@ -34,16 +40,17 @@ def tile_routed_moe_kernel(tc, xT, w_words, w_scales, offs, out):
         tc.psum_pool(name="psum", bufs=1) as psum,
     ):
         lists = keep.tile([P, T // 16], U16, name="lists")
-        x_view = xT.rearrange("(g p u e) n -> g u p e n", g=PASSES, p=P, u=2, e=2)
-        raw = [keep.tile([P, 2, T], F32, name="raw%d" % i) for i in range(SLOTS)]
-        first = x_view[PIECES[0][0], PIECES[0][1]]
-        nc.sync.dma_start(raw[0][:, :, 0:HALF], first[:, :, 0:HALF])
-        nc.sync.dma_start(raw[0][:, :, HALF:T], first[:, :, HALF:T])
+        x_view = xT.rearrange("(g p u v) n -> g u p v n", g=PASSES, p=P, u=2, v=2)
+        raw_pairs = [keep.tile([P, 2, T], F32, name="raw_pairs%d" % i) for i in range(len(PAIR_PIECES))]
+        raw_planes = keep.tile([P, 2, T], F32, name="raw_planes")
+        first = x_view[PAIR_PIECES[0][0], PAIR_PIECES[0][1]]
+        nc.sync.dma_start(raw_pairs[0][:, :, 0:HALF], first[:, :, 0:HALF])
+        nc.sync.dma_start(raw_pairs[0][:, :, HALF:T], first[:, :, HALF:T])
         nc.sync.dma_start(lists[:], offs)
-        for i in range(1, SLOTS - 1):
-            nc.sync.dma_start(raw[i][:], x_view[PIECES[i][0], PIECES[i][1]])
+        for i in range(1, len(PAIR_PIECES)):
+            nc.sync.dma_start(raw_pairs[i][:], x_view[PAIR_PIECES[i][0], PAIR_PIECES[i][1]])
         for v in range(2):
-            nc.sync.dma_start(raw[3][:, v, :], x_view[PIECES[3][0], PIECES[3][1]][:, v, :])
+            nc.sync.dma_start(raw_planes[:, v, :], x_view[PLANE_PIECE[0], PLANE_PIECE[1]][:, v, :])
 
         warm_in = keep.tile([P, 1], F32, name="warm_in")
         warm_out = keep.tile([P, 1], F32, name="warm_out")
@@ -52,17 +59,18 @@ def tile_routed_moe_kernel(tc, xT, w_words, w_scales, offs, out):
 
         w_scale_sb = keep.tile([P, E * PASSES, N], U8, name="w_scale_sb", align_bytes=64)
         nc.vector.memset(w_scale_sb[:].rearrange("p i n -> p (i n)").bitcast(I32), 0)
-        s_view = w_scales.rearrange("e a (q r) n -> r q (e a) n", r=4)
+        scale_rows = w_scales.rearrange("e g (q r) n -> r q (e g) n", r=4)
         for r in range(4):
-            nc.sync.dma_start(w_scale_sb[r:P:32, :, :].bitcast(I32), s_view[r].bitcast(I32))
+            nc.sync.dma_start(w_scale_sb[r:P:32, :, :].bitcast(I32), scale_rows[r].bitcast(I32))
         w_code_sb = keep.tile([P, E * PASSES, 4 * N], U8, name="w_code_sb", align_bytes=64)
-        nc.sync.dma_start(w_code_sb[:], w_words.rearrange("e a p n r -> p (e a) (n r)"))
+        nc.sync.dma_start(w_code_sb[:], w_words.rearrange("e g p n r -> p (e g) (n r)"))
 
-        pairs = keep.tile([P, SLOTS + 1, T, 2], BF16, name="pairs")
-        nc.vector.memset(pairs[:, SLOTS, :, :], 0.0)
-        pair_words = pairs[:].rearrange("p i n e -> p (i n e)").bitcast(U32)
+        sections = len(PAIR_PIECES) + 1
+        pairs = keep.tile([P, sections, T, 2], BF16, name="pairs")
+        nc.vector.memset(pairs[:, sections - 1, :, :], 0.0)
+        pair_words = pairs[:].rearrange("p i n v -> p (i n v)").bitcast(U32)
         planes = keep.tile([P, 2, T], BF16, name="planes")
-        plain = [keep.tile([P, 2, T, 2], BF16, name="plain%d" % g) for g in range(PASSES)]
+        plain = keep.tile([P, 2, T, 2], BF16, name="plain")
         grouped = [keep.tile([P, T, 4], BF16, name="grouped%d" % g, align_bytes=64) for g in range(PASSES)]
         x_code = [keep.tile([P, T], U32, name="x_code%d" % g, align_bytes=64) for g in range(PASSES)]
         x_scale = [keep.tile([P, T], U8, name="x_scale%d" % g, align_bytes=64) for g in range(PASSES)]
@@ -70,86 +78,91 @@ def tile_routed_moe_kernel(tc, xT, w_words, w_scales, offs, out):
         y = [keep.tile([P, HALF], F32, name="y%d" % h) for h in range(2)]
         window_out = keep.tile([P, T], F32, name="window_out")
 
-        def by_gpsimd(out, in_):
-            nc.gpsimd.tensor_scalar(out=out, in0=in_, scalar1=1.0, scalar2=0.0, op0=mybir.AluOpType.mult, op1=mybir.AluOpType.add)
+        def entries(h):
+            return lists[:, h * (HALF // 16):(h + 1) * (HALF // 16)]
 
-        def cast(i):
-            slot = SLOTS - 1 - i
-            for start, for_vector, for_scalar, for_gpsimd in CASTS[i]:
-                for engine, a, b in (
-                    (nc.vector.tensor_copy, start, start + for_vector),
-                    (nc.scalar.copy, start + for_vector, start + for_vector + for_scalar),
-                    (by_gpsimd, start + for_vector + for_scalar, start + for_vector + for_scalar + for_gpsimd),
-                ):
-                    if b > a:
-                        engine(
-                            out=pairs[:, slot, a:b, :].rearrange("p (c i) e -> p c e i", i=4),
-                            in_=raw[i][:, :, a:b].rearrange("p e (c i) -> p c e i", i=4),
-                        )
+        def words_of(g, dtype):
+            return grouped[g][:].rearrange("p s t -> p (s t)").bitcast(dtype).rearrange("p (s u) -> p s u", u=2)
 
-        def gather(i, start, count, width):
-            slot = SLOTS - 1 - i
-            if PIECES[i][0] == LATE:
-                words = grouped[LATE][:].rearrange("p s t -> p (s t)").bitcast(U32).rearrange("p (s u) -> p s u", u=2)[:, :, PIECES[i][1]]
+        def round_on_gpsimd(out, in_):
+            nc.gpsimd.tensor_scalar(out=out, in0=in_, scalar1=1.0, scalar2=0.0, op0=MULT, op1=ADD)
+
+        round_on = {"vector": nc.vector.tensor_copy, "scalar": nc.scalar.copy, "gpsimd": round_on_gpsimd}
+
+        def cast_pairs(i):
+            section = sections - 2 - i
+            for engine, start, count in PAIR_CASTS[i]:
+                tokens = slice(start, start + count)
+                round_on[engine](
+                    out=pairs[:, section, tokens, :].rearrange("p (c i) v -> p c v i", i=4),
+                    in_=raw_pairs[i][:, :, tokens].rearrange("p v (c i) -> p c v i", i=4),
+                )
+
+        def gather_pairs(i):
+            g, u = PAIR_PIECES[i]
+            section = sections - 2 - i
+            if g == EARLY:
+                words = plain[:, u, :, :].rearrange("p s v -> p (s v)").bitcast(U32)
             else:
-                words = plain[PIECES[i][0]][:, PIECES[i][1], :, :].rearrange("p s e -> p (s e)").bitcast(U32)
+                words = words_of(LATE, U32)[:, :, u]
             nc.vector.tensor_copy(
-                words[:, start:start + count],
-                pair_words[:, slot * T:slot * T + width].indirect(lists[:, start // 16:(start + count) // 16]),
+                words[:, 0:T], pair_words[:, section * T:(section + 2) * T].indirect(lists[:, 0:T // 16])
             )
 
-        def interleave(g, start, count):
-            cols = slice(start, start + count)
+        def interleave_early(h):
+            slots = slice(h * HALF, (h + 1) * HALF)
             nc.vector.tensor_copy(
-                out=grouped[g][:, cols, :].rearrange("p s t -> p (s t)").bitcast(I32).rearrange("p (s u) -> p s u", u=2),
-                in_=plain[g][:].rearrange("p u s e -> p (u s e)").bitcast(I32).rearrange("p (u s) -> p s u", u=2)[:, cols, :],
+                out=words_of(EARLY, I32)[:, slots, :],
+                in_=plain[:].rearrange("p u s v -> p (u s v)").bitcast(I32).rearrange("p (u s) -> p s u", u=2)[:, slots, :],
             )
 
-        def quantize(g, start, count):
-            cols = slice(start, start + count)
+        def quantize(g, h):
+            slots = slice(h * HALF, (h + 1) * HALF)
             nc.vector.quantize_mx(
-                out=x_code[g][:, cols].bitcast(FP8X4),
-                scales=x_scale[g][:, cols],
-                in_=grouped[g][:, cols, :].rearrange("p s t -> p (s t)"),
+                out=x_code[g][:, slots].bitcast(FP8X4),
+                scales=x_scale[g][:, slots],
+                in_=grouped[g][:, slots, :].rearrange("p s t -> p (s t)"),
             )
 
-        def multiply(e, a, start, stop):
+        def multiply(e, g, start, stop):
+            slots = slice(e * C, (e + 1) * C)
             nc.tensor.matmul_mx(
                 out=acc[e][:],
-                lhsT=w_code_sb[:, e * PASSES + a, :].bitcast(FP8X4),
-                lhsT_scale=w_scale_sb[:, e * PASSES + a, :],
-                rhs=x_code[a][:, e * C:(e + 1) * C].bitcast(FP8X4),
-                rhs_scale=x_scale[a][:, e * C:(e + 1) * C],
+                lhsT=w_code_sb[:, e * PASSES + g, :].bitcast(FP8X4),
+                lhsT_scale=w_scale_sb[:, e * PASSES + g, :],
+                rhs=x_code[g][:, slots].bitcast(FP8X4),
+                rhs_scale=x_scale[g][:, slots],
                 start=start,
                 stop=stop,
             )
 
-        for i in range(3):
-            cast(i)
-            gather(i, 0, T, 2 * T)
-        by_gpsimd(planes[:, 0, 0:PLANE0_FOR_GPSIMD], raw[3][:, 0, 0:PLANE0_FOR_GPSIMD])
-        nc.scalar.copy(out=planes[:, 0, PLANE0_FOR_GPSIMD:T], in_=raw[3][:, 0, PLANE0_FOR_GPSIMD:T])
-        by_gpsimd(planes[:, 1, :], raw[3][:, 1, :])
+        for i in range(len(PAIR_PIECES)):
+            cast_pairs(i)
+            gather_pairs(i)
+
+        round_on_gpsimd(planes[:, 0, 0:PLANE0_FOR_GPSIMD], raw_planes[:, 0, 0:PLANE0_FOR_GPSIMD])
+        nc.scalar.copy(out=planes[:, 0, PLANE0_FOR_GPSIMD:T], in_=raw_planes[:, 0, PLANE0_FOR_GPSIMD:T])
+        round_on_gpsimd(planes[:, 1, :], raw_planes[:, 1, :])
+
         for h in range(2):
-            interleave(EARLY, h * HALF, HALF)
+            interleave_early(h)
         for h in range(2):
-            quantize(EARLY, h * HALF, HALF)
+            quantize(EARLY, h)
             for e in (2 * h, 2 * h + 1):
                 multiply(e, EARLY, True, False)
+
         both_planes = planes[:].rearrange("p v n -> p (v n)")
         for h in range(2):
             for v in range(2):
+                window = both_planes if (h, v) == (1, 0) else planes[:, v, :]
                 nc.scalar.activation(
-                    grouped[LATE][:, h * HALF:(h + 1) * HALF, 2 * PIECES[3][1] + v],
-                    (both_planes if (h, v) == (1, 0) else planes[:, v, :]).indirect(lists[:, h * (HALF // 16):(h + 1) * (HALF // 16)]),
-                    COPY,
+                    grouped[LATE][:, h * HALF:(h + 1) * HALF, 2 * PLANE_PIECE[1] + v], window.indirect(entries(h)), COPY
                 )
-            quantize(LATE, h * HALF, HALF)
+            quantize(LATE, h)
+
         for e in range(E):
             multiply(e, LATE, False, True)
             nc.scalar.copy(out=y[e // 2][:, (e % 2) * C:(e % 2 + 1) * C], in_=acc[e][:])
         for h in range(2):
-            nc.vector.tensor_copy(
-                window_out[:].indirect(lists[:, h * (HALF // 16):(h + 1) * (HALF // 16)]), y[h][:]
-            )
+            nc.vector.tensor_copy(window_out[:].indirect(entries(h)), y[h][:])
         nc.sync.dma_start(out, window_out[:])

@@ -26,7 +26,7 @@ PAIR_PIECES = ((LATE, 0), (EARLY, 0), (EARLY, 1))
 PLANE_PIECE = (LATE, 1)
 
 PAIR_CASTS = (
-    (("vector", 0, 176), ("scalar", 176, 80), ("vector", 256, 176), ("scalar", 432, 80)),
+    (("vector", 0, 176), ("scalar", 176, 80), ("vector", 256, 88), ("scalar", 344, 40), ("vector", 384, 88), ("scalar", 472, 40)),
     (("scalar", 0, 384), ("gpsimd", 384, 128)),
     (("scalar", 0, 368), ("gpsimd", 368, 144)),
 )
@@ -44,8 +44,8 @@ def tile_routed_moe_kernel(tc, xT, w_words, w_scales, offs, out):
         raw_pairs = [keep.tile([P, 2, T], F32, name="raw_pairs%d" % i) for i in range(len(PAIR_PIECES))]
         raw_planes = keep.tile([P, 2, T], F32, name="raw_planes")
         first = x_view[PAIR_PIECES[0][0], PAIR_PIECES[0][1]]
-        nc.sync.dma_start(raw_pairs[0][:, :, 0:HALF], first[:, :, 0:HALF])
-        nc.sync.dma_start(raw_pairs[0][:, :, HALF:T], first[:, :, HALF:T])
+        for a, b in ((0, 256), (256, 384), (384, 512)):
+            nc.sync.dma_start(raw_pairs[0][:, :, a:b], first[:, :, a:b])
         nc.sync.dma_start(lists[:], offs)
         for i in range(1, len(PAIR_PIECES)):
             nc.sync.dma_start(raw_pairs[i][:], x_view[PAIR_PIECES[i][0], PAIR_PIECES[i][1]])

import concourse.mybir as mybir

FLOPS = 2 * 1024 * 128 * 512

F32 = mybir.dt.float32
BF16 = mybir.dt.bfloat16
I32 = mybir.dt.int32
U32 = mybir.dt.uint32
U16 = mybir.dt.uint16
U8 = mybir.dt.uint8
FP8X4 = mybir.dt.float8_e4m3fn_x4
COPY = mybir.ActivationFunctionType.Copy
MULT = mybir.AluOpType.mult
ADD = mybir.AluOpType.add

P = 128
T = 512
E = 4
C = 128
N = 128
PASSES = 2
HALF = T // 2

EARLY, LATE = 1, 0
PAIR_PIECES = ((LATE, 0), (EARLY, 0), (EARLY, 1))
PLANE_PIECE = (LATE, 1)

PAIR_CASTS = (
    (("vector", 0, 176), ("scalar", 176, 80), ("vector", 256, 88), ("scalar", 344, 40), ("vector", 384, 88), ("scalar", 472, 40)),
    (("scalar", 0, 384), ("gpsimd", 384, 128)),
    (("scalar", 0, 368), ("gpsimd", 368, 144)),
)
PLANE0_FOR_GPSIMD = 304


def tile_routed_moe_kernel(tc, xT, w_words, w_scales, offs, out):
    nc = tc.nc
    with (
        tc.tile_pool(name="keep", bufs=1) as keep,
        tc.psum_pool(name="psum", bufs=1) as psum,
    ):
        lists = keep.tile([P, T // 16], U16, name="lists")
        x_view = xT.rearrange("(g p u v) n -> g u p v n", g=PASSES, p=P, u=2, v=2)
        raw_pairs = [keep.tile([P, 2, T], F32, name="raw_pairs%d" % i) for i in range(len(PAIR_PIECES))]
        raw_planes = keep.tile([P, 2, T], F32, name="raw_planes")
        first = x_view[PAIR_PIECES[0][0], PAIR_PIECES[0][1]]
        for a, b in ((0, 256), (256, 384), (384, 512)):
            nc.sync.dma_start(raw_pairs[0][:, :, a:b], first[:, :, a:b])
        nc.sync.dma_start(lists[:], offs)
        for i in range(1, len(PAIR_PIECES)):
            nc.sync.dma_start(raw_pairs[i][:], x_view[PAIR_PIECES[i][0], PAIR_PIECES[i][1]])
        for v in range(2):
            nc.sync.dma_start(raw_planes[:, v, :], x_view[PLANE_PIECE[0], PLANE_PIECE[1]][:, v, :])

        warm_in = keep.tile([P, 1], F32, name="warm_in")
        warm_out = keep.tile([P, 1], F32, name="warm_out")
        nc.vector.memset(warm_in[:], 0.0)
        nc.scalar.copy(out=warm_out[:], in_=warm_in[:])

        w_scale_sb = keep.tile([P, E * PASSES, N], U8, name="w_scale_sb", align_bytes=64)
        nc.vector.memset(w_scale_sb[:].rearrange("p i n -> p (i n)").bitcast(I32), 0)
        scale_rows = w_scales.rearrange("e g (q r) n -> r q (e g) n", r=4)
        for r in range(4):
            nc.sync.dma_start(w_scale_sb[r:P:32, :, :].bitcast(I32), scale_rows[r].bitcast(I32))
        w_code_sb = keep.tile([P, E * PASSES, 4 * N], U8, name="w_code_sb", align_bytes=64)
        nc.sync.dma_start(w_code_sb[:], w_words.rearrange("e g p n r -> p (e g) (n r)"))

        sections = len(PAIR_PIECES) + 1
        pairs = keep.tile([P, sections, T, 2], BF16, name="pairs")
        nc.vector.memset(pairs[:, sections - 1, :, :], 0.0)
        pair_words = pairs[:].rearrange("p i n v -> p (i n v)").bitcast(U32)
        planes = keep.tile([P, 2, T], BF16, name="planes")
        plain = keep.tile([P, 2, T, 2], BF16, name="plain")
        grouped = [keep.tile([P, T, 4], BF16, name="grouped%d" % g, align_bytes=64) for g in range(PASSES)]
        x_code = [keep.tile([P, T], U32, name="x_code%d" % g, align_bytes=64) for g in range(PASSES)]
        x_scale = [keep.tile([P, T], U8, name="x_scale%d" % g, align_bytes=64) for g in range(PASSES)]
        acc = [psum.tile([P, C], F32, name="acc%d" % e) for e in range(E)]
        y = [keep.tile([P, HALF], F32, name="y%d" % h) for h in range(2)]
        window_out = keep.tile([P, T], F32, name="window_out")

        def entries(h):
            return lists[:, h * (HALF // 16):(h + 1) * (HALF // 16)]

        def words_of(g, dtype):
            return grouped[g][:].rearrange("p s t -> p (s t)").bitcast(dtype).rearrange("p (s u) -> p s u", u=2)

        def round_on_gpsimd(out, in_):
            nc.gpsimd.tensor_scalar(out=out, in0=in_, scalar1=1.0, scalar2=0.0, op0=MULT, op1=ADD)

        round_on = {"vector": nc.vector.tensor_copy, "scalar": nc.scalar.copy, "gpsimd": round_on_gpsimd}

        def cast_pairs(i):
            section = sections - 2 - i
            for engine, start, count in PAIR_CASTS[i]:
                tokens = slice(start, start + count)
                round_on[engine](
                    out=pairs[:, section, tokens, :].rearrange("p (c i) v -> p c v i", i=4),
                    in_=raw_pairs[i][:, :, tokens].rearrange("p v (c i) -> p c v i", i=4),
                )

        def gather_pairs(i):
            g, u = PAIR_PIECES[i]
            section = sections - 2 - i
            if g == EARLY:
                words = plain[:, u, :, :].rearrange("p s v -> p (s v)").bitcast(U32)
            else:
                words = words_of(LATE, U32)[:, :, u]
            nc.vector.tensor_copy(
                words[:, 0:T], pair_words[:, section * T:(section + 2) * T].indirect(lists[:, 0:T // 16])
            )

        def interleave_early(h):
            slots = slice(h * HALF, (h + 1) * HALF)
            nc.vector.tensor_copy(
                out=words_of(EARLY, I32)[:, slots, :],
                in_=plain[:].rearrange("p u s v -> p (u s v)").bitcast(I32).rearrange("p (u s) -> p s u", u=2)[:, slots, :],
            )

        def quantize(g, h):
            slots = slice(h * HALF, (h + 1) * HALF)
            nc.vector.quantize_mx(
                out=x_code[g][:, slots].bitcast(FP8X4),
                scales=x_scale[g][:, slots],
                in_=grouped[g][:, slots, :].rearrange("p s t -> p (s t)"),
            )

        def multiply(e, g, start, stop):
            slots = slice(e * C, (e + 1) * C)
            nc.tensor.matmul_mx(
                out=acc[e][:],
                lhsT=w_code_sb[:, e * PASSES + g, :].bitcast(FP8X4),
                lhsT_scale=w_scale_sb[:, e * PASSES + g, :],
                rhs=x_code[g][:, slots].bitcast(FP8X4),
                rhs_scale=x_scale[g][:, slots],
                start=start,
                stop=stop,
            )

        for i in range(len(PAIR_PIECES)):
            cast_pairs(i)
            gather_pairs(i)

        round_on_gpsimd(planes[:, 0, 0:PLANE0_FOR_GPSIMD], raw_planes[:, 0, 0:PLANE0_FOR_GPSIMD])
        nc.scalar.copy(out=planes[:, 0, PLANE0_FOR_GPSIMD:T], in_=raw_planes[:, 0, PLANE0_FOR_GPSIMD:T])
        round_on_gpsimd(planes[:, 1, :], raw_planes[:, 1, :])

        for h in range(2):
            interleave_early(h)
        for h in range(2):
            quantize(EARLY, h)
            for e in (2 * h, 2 * h + 1):
                multiply(e, EARLY, True, False)

        both_planes = planes[:].rearrange("p v n -> p (v n)")
        for h in range(2):
            for v in range(2):
                window = both_planes if (h, v) == (1, 0) else planes[:, v, :]
                nc.scalar.activation(
                    grouped[LATE][:, h * HALF:(h + 1) * HALF, 2 * PLANE_PIECE[1] + v], window.indirect(entries(h)), COPY
                )
            quantize(LATE, h)

        for e in range(E):
            multiply(e, LATE, False, True)
            nc.scalar.copy(out=y[e // 2][:, (e % 2) * C:(e % 2 + 1) * C], in_=acc[e][:])
        for h in range(2):
            nc.vector.tensor_copy(window_out[:].indirect(entries(h)), y[h][:])
        nc.sync.dma_start(out, window_out[:])
